import numpy as np
import ml_dtypes


def mxq(x, axis, fmt="e4m3"):
    dtype, down = {"e4m3": (ml_dtypes.float8_e4m3fn, 7), "e5m2": (ml_dtypes.float8_e5m2, 14)}[fmt]
    v = np.moveaxis(np.asarray(x, np.float32).astype(ml_dtypes.bfloat16).astype(np.float64), axis, -1)
    blocks = v.reshape(v.shape[:-1] + (-1, 32))
    amax = np.abs(blocks).max(-1, keepdims=True)
    byte = np.maximum(np.where(amax > 0, np.frexp(amax)[1] - 1 + 127, 0) - down, 1)
    scale = np.exp2(byte - 127.0)
    codes = (blocks / scale).astype(np.float32).astype(dtype).astype(np.float64)
    return np.moveaxis((codes * scale).reshape(v.shape), -1, axis)


WIDE = False


def mx_kscale(k):
    if not WIDE:
        return np.ones(k)
    levels = np.array([10, -10, 5, -5, 0])
    if k % 512:
        return np.exp2(np.random.permutation(np.resize(levels, k // 32))).repeat(32)
    a = np.empty((k // 512, 16))
    for p in range(k // 512):
        a[p, :8] = np.random.permutation(np.resize(levels, 8))
        for g in range(8):
            far = levels[np.abs(levels - a[p, g]) >= 10]
            a[p, g + 8] = far[np.random.randint(len(far))]
    return np.exp2(a.ravel()).repeat(32)


def f64(x):
    return np.asarray(x).astype(np.float64)


def striped(idx):
    return np.tile(idx.reshape(-1, 16).T, (8, 1)).astype(np.uint16)


def unstriped(offs):
    return offs[:16].T.reshape(-1).astype(np.int64)


def pack_weight(w):
    k, n = w.shape
    w = f64(np.asarray(w, np.float32).astype(ml_dtypes.bfloat16)).reshape(k // 32, 32, n)
    amax = np.abs(w).max(1)
    byte = np.clip(np.where(amax > 0, np.frexp(amax)[1] - 1 + 127 - 7, 1), 1, 254)
    scaled = (w * np.exp2(127.0 - byte)[:, None, :]).reshape(k, n).astype(np.float32)
    words = np.ascontiguousarray(scaled.reshape(k // 512, 128, 4, n).transpose(0, 1, 3, 2)).astype(ml_dtypes.float8_e4m3fn).view(np.uint8)
    return words, np.ascontiguousarray(byte.astype(np.uint8).reshape(k // 512, 16, n))


def unpack_weight(words, scales):
    g, p, n, _ = words.shape
    vals = np.ascontiguousarray(words).view(ml_dtypes.float8_e4m3fn).astype(np.float64) * np.repeat(np.exp2(scales.astype(np.float64) - 127.0), 8, axis=1)[..., None]
    return vals.transpose(0, 1, 3, 2).reshape(g * 512, n)


def relu(v):
    return np.maximum(v, 0.0)


def sigmoid(v):
    return 1.0 / (1.0 + np.exp(-np.maximum(v, -700.0)))


K, T, S, D, H, Z, W = 512, 2048, 512, 2, 512, 512, 1024


def setup_inputs():
    n = np.random.standard_normal
    s = mx_kscale(K)[:, None]
    u = mx_kscale(H)
    packed_xT = pack_weight(n((K, T)) * s)
    packed_eT = pack_weight(n((K, W)) * s)
    return {
        "x_words": packed_xT[0],
        "x_scales": packed_xT[1],
        "w1": (n((K, H)) / np.sqrt(K) / s).astype(np.float32),
        "e_words": packed_eT[0],
        "e_scales": packed_eT[1],
        "w2": (n((K, H)) / np.sqrt(K) / s).astype(np.float32),
        "w3": (n((K, H)) / np.sqrt(K) / s).astype(np.float32),
        "unit": (np.random.uniform(0.6, 1.4, (H, 1)) * u[:, None]).astype(np.float32),
        "unit2": (np.random.uniform(0.6, 1.4, (H, 1)) / np.sqrt(H) / u[:, None]).astype(np.float32),
        "offs": striped(np.random.permutation(T)[:S]),
        "pok": striped(np.random.permutation(W)[:Z]),
        "adj": striped(np.random.permutation(Z)),
        "alo": striped(np.random.permutation(Z)),
    }


def reference(x_words, x_scales, w1, e_words, e_scales, w2, w3, unit, unit2, offs, pok, adj, alo):
    xq = unpack_weight(x_words, x_scales)[:, unstriped(offs)]
    y = mxq(f64(w1), 0, "e4m3").T @ xq
    ry = relu(y)
    drug = ry.reshape(len(ry), -1, D).sum(axis=2)
    hid = f64(unit) * drug
    e_pok = unpack_weight(e_words, e_scales)[:, unstriped(pok)]
    ye = mxq(f64(w2), 0, "e4m3").T @ e_pok
    yw = mxq(f64(w3), 0, "e4m3").T @ e_pok
    wa = yw[:, unstriped(adj)]
    pock = ye - (0.7 * wa)
    hid2 = f64(unit2) * pock
    sc = mxq(hid, 0, "e4m3").T @ mxq(hid2, 0, "e4m3")
    allo = sc * (sigmoid(sc[:, unstriped(alo)]))
    top = allo.max(axis=1, keepdims=True)
    return allo / (np.abs(top) + 0.5)

@@ -1,0 +1,242 @@
+from contextlib import ExitStack
+
+import concourse.mybir as mybir
+
+K, T, S, H, Z, W = 512, 2048, 512, 512, 512, 1024
+V = S // 2
+
+F32 = mybir.dt.float32
+BF16 = mybir.dt.bfloat16
+I32 = mybir.dt.int32
+U32 = mybir.dt.uint32
+U16 = mybir.dt.uint16
+U8 = mybir.dt.uint8
+FP8X4 = mybir.dt.float8_e4m3fn_x4
+ALU = mybir.AluOpType
+ACT = mybir.ActivationFunctionType
+AXIS = mybir.AxisListType
+
+P = 128
+PACK = 4
+HALF = 256
+LIST_COLS = HALF // 16
+
+FLOPS = 2 * K * H * (S + 2 * Z) + 2 * H * V * Z
+
+
+def tile_picked_ydrgtg_rel_p_kernel(
+    tc, x_words, x_scales, w1, e_words, e_scales, w2, w3, unit, unit2, offs, pok, adj, alo, out
+):
+    nc = tc.nc
+    with ExitStack() as ctx:
+        keep = ctx.enter_context(tc.tile_pool(name="keep", bufs=1))
+        psum = ctx.enter_context(tc.psum_pool(name="psum", bufs=1))
+
+        def sb(name, shape, dtype):
+            return keep.tile(shape, dtype, name=name, align_bytes=64)
+
+        def bank(tag, shape, name):
+            return psum.tile(shape, F32, name=name, tag=tag)
+
+        def load_list(name, src):
+            tile = keep.tile([P, 32], U16, name=name)
+            nc.sync.dma_start(tile[:], src)
+            return tile
+
+        def load_words(name, src, width):
+            tile = sb(name, [P, width], I32)
+            nc.sync.dma_start(tile[:], src[0].rearrange("p n t -> p (n t)").bitcast(I32))
+            return tile
+
+        def load_scales(name, src, width, queue):
+            tile = sb(name, [P, width], U8)
+            nc.vector.memset(tile[:].bitcast(I32), 0)
+            for q in range(4):
+                queue.dma_start(tile[32 * q : 32 * q + 4, :].bitcast(I32), src[0, 4 * q : 4 * q + 4, :].bitcast(I32))
+            return tile
+
+        def load_weight(name, src):
+            tile = sb(name, [P, PACK, H], F32)
+            nc.sync.dma_start(tile[:], src.rearrange("(p j) c -> p j c", j=PACK))
+            return tile
+
+        def load_unit(name, src):
+            tile = sb(name, [P, PACK], F32)
+            nc.gpsimd.dma_start(tile[:], src.rearrange("(p t) o -> p (t o)", t=PACK))
+            return tile
+
+        def deal_weight(name, raw, scalar_cols):
+            dealt = sb(name, [P, PACK, P, PACK], BF16)
+            dst = dealt[:].rearrange("p t m j -> p m j t")
+            src = raw[:].rearrange("p j (m t) -> p m j t", t=PACK)
+            if scalar_cols > 0:
+                nc.scalar.copy(dst[:, :scalar_cols], src[:, :scalar_cols])
+            if scalar_cols < P:
+                nc.vector.tensor_copy(dst[:, scalar_cols:], src[:, scalar_cols:])
+            return dealt
+
+        def quantize(name, flat, pieces):
+            width = flat.shape[1] // PACK
+            codes = sb(name + "_codes", [P, width], U32)
+            scales = sb(name + "_scales", [P, width], U8)
+            step = width // pieces
+            for c in range(0, width, step):
+                nc.vector.quantize_mx(
+                    out=codes[:, c : c + step].bitcast(FP8X4),
+                    scales=scales[:, c : c + step],
+                    in_=flat[:, PACK * c : PACK * (c + step)],
+                )
+            return codes, scales
+
+        def product(dst, stat, stat_cols, mov, mov_cols):
+            nc.tensor.matmul_mx(
+                out=dst,
+                lhsT=stat[0][:, stat_cols].bitcast(FP8X4),
+                lhsT_scale=stat[1][:, stat_cols],
+                rhs=mov[0][:, mov_cols].bitcast(FP8X4),
+                rhs_scale=mov[1][:, mov_cols],
+                start=True,
+                stop=True,
+            )
+
+        def tile_cols(t):
+            return slice(t * P, (t + 1) * P)
+
+        def half_cols(h):
+            return slice(h * HALF, (h + 1) * HALF)
+
+        def half_list(tile, h):
+            return tile[:, h * LIST_COLS : (h + 1) * LIST_COLS]
+
+        pok_t = load_list("pok_t", pok)
+        offs_t = load_list("offs_t", offs)
+        e_table = load_words("e_table", e_words, W)
+        e_bytes = load_scales("e_bytes", e_scales, W, nc.scalar)
+        w3_raw = load_weight("w3_raw", w3)
+        unit_t = load_unit("unit_t", unit)
+        unit2_t = load_unit("unit2_t", unit2)
+        x_bytes = load_scales("x_bytes", x_scales, T, nc.gpsimd)
+        w2_raw = load_weight("w2_raw", w2)
+        adj_t = load_list("adj_t", adj)
+        w1_raw = load_weight("w1_raw", w1)
+        x_table = load_words("x_table", x_words, T)
+        alo_t = load_list("alo_t", alo)
+
+        step01 = sb("step01", [P, PACK], F32)
+        sign = sb("sign", [P, PACK], F32)
+        unit_abs = sb("unit_abs", [P, PACK], F32)
+        ye_gain = sb("ye_gain", [P, PACK], F32)
+        yw_gain = sb("yw_gain", [P, PACK], F32)
+        nc.gpsimd.tensor_scalar(step01[:], unit_t[:], 0.0, None, ALU.is_ge)
+        nc.gpsimd.tensor_scalar(sign[:], step01[:], 2.0, -1.0, ALU.mult, ALU.add)
+        nc.gpsimd.tensor_tensor(ye_gain[:], unit2_t[:], sign[:], ALU.mult)
+        nc.gpsimd.tensor_scalar(yw_gain[:], ye_gain[:], -0.7, 0.0, ALU.mult, ALU.add)
+        nc.gpsimd.tensor_tensor(unit_abs[:], unit_t[:], sign[:], ALU.mult)
+
+        e_codes = sb("e_codes", [P, Z], U32)
+        e_planes = sb("e_planes", [P, Z], U8)
+        nc.vector.tensor_copy(e_planes[:], e_bytes[:].indirect(pok_t[:]))
+        nc.vector.tensor_copy(e_codes[:], e_table[:].bitcast(U32).indirect(pok_t[:]))
+        e_mx = (e_codes, e_planes)
+        x_codes = sb("x_codes", [P, S], U32)
+        x_planes = sb("x_planes", [P, S], U8)
+        nc.vector.tensor_copy(x_planes[:], x_bytes[:].indirect(offs_t[:]))
+        x_mx = (x_codes, x_planes)
+
+        w3_dealt = deal_weight("w3_dealt", w3_raw, 64)
+        w3_mx = quantize("w3", w3_dealt[:].rearrange("p t m j -> p (t m j)"), 2)
+        yw = []
+        for t in range(PACK):
+            acc = bank("a%d" % t, [P, Z], "yw_acc%d" % t)
+            product(acc[:], w3_mx, tile_cols(t), e_mx, slice(0, Z))
+            rows = sb("yw%d" % t, [P, Z], F32)
+            nc.scalar.activation(rows[:], acc[:], ACT.Copy, scale=yw_gain[:, t : t + 1])
+            yw.append(rows)
+
+        w2_dealt = deal_weight("w2_dealt", w2_raw, 0)
+        w2_mx = quantize("w2", w2_dealt[:].rearrange("p t m j -> p (t m j)"), 1)
+        ye = []
+        for t in range(PACK):
+            acc = bank("b%d" % t, [P, Z], "ye_acc%d" % t)
+            product(acc[:], w2_mx, tile_cols(t), e_mx, slice(0, Z))
+            ye.append(acc)
+
+        wa = []
+        for t in range(PACK):
+            rows = sb("wa%d" % t, [P, Z], F32)
+            for h in range(2):
+                nc.scalar.activation(rows[:, half_cols(h)], yw[t][:].indirect(half_list(adj_t, h)), ACT.Copy)
+            wa.append(rows)
+
+        w1_dealt = deal_weight("w1_dealt", w1_raw, 0)
+        w1_mx = quantize("w1", w1_dealt[:].rearrange("p t m j -> p (t m j)"), 1)
+
+        hid2_rows = sb("hid2_rows", [P, PACK, Z], BF16)
+        for t in range(PACK):
+            nc.vector.scalar_tensor_tensor(
+                hid2_rows[:, t, :], ye[t][:], ye_gain[:, t : t + 1], wa[t][:], ALU.mult, ALU.add
+            )
+            if t < 2:
+                nc.vector.tensor_copy(x_codes[:, half_cols(t)], x_table[:].bitcast(U32).indirect(half_list(offs_t, t)))
+
+        rect = []
+        for h in range(2):
+            rows = sb("rect%d" % h, [P, 2, PACK, P], F32)
+            for pair in range(2):
+                acc = bank("a%d" % (2 * h + pair), [P, 2, HALF], "y_acc%d" % (2 * h + pair))
+                for u in range(2):
+                    product(acc[:, u, :], w1_mx, tile_cols(2 * pair + u), x_mx, half_cols(h))
+                for u in range(2):
+                    t = 2 * pair + u
+                    nc.scalar.activation(
+                        rows[:, :, t, :],
+                        acc[:, u, :].rearrange("p (v d) -> p d v", d=2),
+                        ACT.Relu,
+                        scale=unit_abs[:, t : t + 1],
+                    )
+            rect.append(rows)
+
+        hid2 = sb("hid2", [P, Z, PACK], BF16)
+        nc.vector.tensor_copy(
+            hid2[:].rearrange("p (c i) t -> p c t i", i=4), hid2_rows[:].rearrange("p t (c i) -> p c t i", i=4)
+        )
+        hid = []
+        for h in range(2):
+            both = sb("hid%d" % h, [P, P, PACK], BF16)
+            hid.append(both)
+
+        def add_pair(h):
+            nc.vector.tensor_tensor(
+                hid[h][:].rearrange("p (c i) t -> p c t i", i=4),
+                rect[h][:, 0].rearrange("p t (c i) -> p c t i", i=4),
+                rect[h][:, 1].rearrange("p t (c i) -> p c t i", i=4),
+                ALU.add,
+            )
+
+        add_pair(0)
+        hid2_mx = quantize("hid2", hid2[:].rearrange("p e t -> p (e t)"), 1)
+        hid_mx = [quantize("hid0", hid[0][:].rearrange("p v t -> p (v t)"), 1)]
+        add_pair(1)
+        hid_mx.append(quantize("hid1", hid[1][:].rearrange("p v t -> p (v t)"), 1))
+
+        for h in range(2):
+            acc = bank("b%d" % h, [P, Z], "sc_acc%d" % h)
+            product(acc[:], hid_mx[h], slice(0, P), hid2_mx, slice(0, Z))
+            sc = sb("sc%d" % h, [P, Z], F32)
+            nc.scalar.copy(sc[:], acc[:])
+            gate = sb("gate%d" % h, [P, Z], F32)
+            allo = sb("allo%d" % h, [P, Z], F32)
+            for g in range(2):
+                nc.scalar.activation(gate[:, half_cols(g)], sc[:].indirect(half_list(alo_t, g)), ACT.Sigmoid)
+                nc.vector.tensor_tensor(allo[:, half_cols(g)], gate[:, half_cols(g)], sc[:, half_cols(g)], ALU.mult)
+            top = sb("top%d" % h, [P, 1], F32)
+            low = sb("low%d" % h, [P, 1], F32)
+            den = sb("den%d" % h, [P, 1], F32)
+            inv = sb("inv%d" % h, [P, 1], F32)
+            nc.vector.tensor_reduce(top[:], allo[:], AXIS.X, ALU.max)
+            nc.vector.tensor_scalar(low[:], top[:], -1.0, 0.5, ALU.mult, ALU.add)
+            nc.vector.scalar_tensor_tensor(den[:], top[:], 0.5, low[:], ALU.add, ALU.max)
+            nc.vector.reciprocal(inv[:], den[:])
+            res = sb("res%d" % h, [P, Z], F32)
+            nc.vector.tensor_scalar(res[:], allo[:], inv[:, 0:1], None, ALU.mult)
+            nc.sync.dma_start(out[h * P : (h + 1) * P, :], res[:])

@@ -32,8 +32,8 @@ def tile_picked_ydrgtg_rel_p_kernel(
         keep = ctx.enter_context(tc.tile_pool(name="keep", bufs=1))
         psum = ctx.enter_context(tc.psum_pool(name="psum", bufs=1))
 
-        def sb(name, shape, dtype):
-            return keep.tile(shape, dtype, name=name, align_bytes=64)
+        def sb(name, shape, dtype, tag=""):
+            return keep.tile(shape, dtype, name=name, tag=tag or name, align_bytes=64)
 
         def bank(tag, shape, name):
             return psum.tile(shape, F32, name=name, tag=tag)
@@ -50,7 +50,7 @@ def tile_picked_ydrgtg_rel_p_kernel(
 
         def load_scales(name, src, width, queue):
             tile = sb(name, [P, width], U8)
-            nc.vector.memset(tile[:].bitcast(I32), 0)
+            nc.gpsimd.memset(tile[:].bitcast(I32), 0)
             for q in range(4):
                 queue.dma_start(tile[32 * q : 32 * q + 4, :].bitcast(I32), src[0, 4 * q : 4 * q + 4, :].bitcast(I32))
             return tile
@@ -62,7 +62,7 @@ def tile_picked_ydrgtg_rel_p_kernel(
 
         def load_unit(name, src):
             tile = sb(name, [P, PACK], F32)
-            nc.gpsimd.dma_start(tile[:], src.rearrange("(p t) o -> p (t o)", t=PACK))
+            nc.sync.dma_start(tile[:], src.rearrange("(p t) o -> p (t o)", t=PACK))
             return tile
 
         def deal_weight(name, raw, scalar_cols):
@@ -111,39 +111,50 @@ def tile_picked_ydrgtg_rel_p_kernel(
         pok_t = load_list("pok_t", pok)
         offs_t = load_list("offs_t", offs)
         e_table = load_words("e_table", e_words, W)
-        e_bytes = load_scales("e_bytes", e_scales, W, nc.scalar)
+        e_bytes = load_scales("e_bytes", e_scales, W, nc.sync)
         w3_raw = load_weight("w3_raw", w3)
         unit_t = load_unit("unit_t", unit)
         unit2_t = load_unit("unit2_t", unit2)
-        x_bytes = load_scales("x_bytes", x_scales, T, nc.gpsimd)
+        x_bytes = load_scales("x_bytes", x_scales, T, nc.sync)
         w2_raw = load_weight("w2_raw", w2)
         adj_t = load_list("adj_t", adj)
         w1_raw = load_weight("w1_raw", w1)
         x_table = load_words("x_table", x_words, T)
         alo_t = load_list("alo_t", alo)
 
+        warm_in = sb("warm_in", [P, 1], F32)
+        warm_out = sb("warm_out", [P, 1], F32)
+        nc.gpsimd.memset(warm_in[:], 0.0)
+        nc.scalar.activation(warm_out[:], warm_in[:], ACT.Sigmoid)
+
         step01 = sb("step01", [P, PACK], F32)
         sign = sb("sign", [P, PACK], F32)
         unit_abs = sb("unit_abs", [P, PACK], F32)
         ye_gain = sb("ye_gain", [P, PACK], F32)
         yw_gain = sb("yw_gain", [P, PACK], F32)
+        sign07 = sb("sign07", [P, PACK], F32)
         nc.gpsimd.tensor_scalar(step01[:], unit_t[:], 0.0, None, ALU.is_ge)
+        nc.gpsimd.tensor_scalar(sign07[:], step01[:], -1.4, 0.7, ALU.mult, ALU.add)
+        nc.gpsimd.tensor_tensor(yw_gain[:], unit2_t[:], sign07[:], ALU.mult)
         nc.gpsimd.tensor_scalar(sign[:], step01[:], 2.0, -1.0, ALU.mult, ALU.add)
         nc.gpsimd.tensor_tensor(ye_gain[:], unit2_t[:], sign[:], ALU.mult)
-        nc.gpsimd.tensor_scalar(yw_gain[:], ye_gain[:], -0.7, 0.0, ALU.mult, ALU.add)
-        nc.gpsimd.tensor_tensor(unit_abs[:], unit_t[:], sign[:], ALU.mult)
+        nc.scalar.activation(unit_abs[:], unit_t[:], ACT.Abs)
+        top_and_half = []
+        for h in range(2):
+            pair = sb("top_and_half%d" % h, [P, 2], F32)
+            nc.vector.memset(pair[:], 0.5)
+            top_and_half.append(pair)
 
         e_codes = sb("e_codes", [P, Z], U32)
         e_planes = sb("e_planes", [P, Z], U8)
-        nc.vector.tensor_copy(e_planes[:], e_bytes[:].indirect(pok_t[:]))
         nc.vector.tensor_copy(e_codes[:], e_table[:].bitcast(U32).indirect(pok_t[:]))
+        nc.vector.tensor_copy(e_planes[:], e_bytes[:].indirect(pok_t[:]))
         e_mx = (e_codes, e_planes)
         x_codes = sb("x_codes", [P, S], U32)
         x_planes = sb("x_planes", [P, S], U8)
-        nc.vector.tensor_copy(x_planes[:], x_bytes[:].indirect(offs_t[:]))
         x_mx = (x_codes, x_planes)
 
-        w3_dealt = deal_weight("w3_dealt", w3_raw, 64)
+        w3_dealt = deal_weight("w3_dealt", w3_raw, 44)
         w3_mx = quantize("w3", w3_dealt[:].rearrange("p t m j -> p (t m j)"), 2)
         yw = []
         for t in range(PACK):
@@ -153,6 +164,7 @@ def tile_picked_ydrgtg_rel_p_kernel(
             nc.scalar.activation(rows[:], acc[:], ACT.Copy, scale=yw_gain[:, t : t + 1])
             yw.append(rows)
 
+        nc.vector.tensor_copy(x_planes[:], x_bytes[:].indirect(offs_t[:]))
         w2_dealt = deal_weight("w2_dealt", w2_raw, 0)
         w2_mx = quantize("w2", w2_dealt[:].rearrange("p t m j -> p (t m j)"), 1)
         ye = []
@@ -161,23 +173,44 @@ def tile_picked_ydrgtg_rel_p_kernel(
             product(acc[:], w2_mx, tile_cols(t), e_mx, slice(0, Z))
             ye.append(acc)
 
-        wa = []
-        for t in range(PACK):
-            rows = sb("wa%d" % t, [P, Z], F32)
-            for h in range(2):
-                nc.scalar.activation(rows[:, half_cols(h)], yw[t][:].indirect(half_list(adj_t, h)), ACT.Copy)
-            wa.append(rows)
+        wa = [[], []]
+        for h in range(2):
+            for t in range(PACK):
+                rows = sb("wa%d_%d" % (h, t), [P, HALF], F32)
+                nc.scalar.activation(rows[:], yw[t][:].indirect(half_list(adj_t, h)), ACT.Copy)
+                wa[h].append(rows)
 
         w1_dealt = deal_weight("w1_dealt", w1_raw, 0)
         w1_mx = quantize("w1", w1_dealt[:].rearrange("p t m j -> p (t m j)"), 1)
 
-        hid2_rows = sb("hid2_rows", [P, PACK, Z], BF16)
-        for t in range(PACK):
-            nc.vector.scalar_tensor_tensor(
-                hid2_rows[:, t, :], ye[t][:], ye_gain[:, t : t + 1], wa[t][:], ALU.mult, ALU.add
+        hid2_codes = sb("hid2_codes", [P, Z], U32)
+        hid2_planes = sb("hid2_planes", [P, Z], U8)
+        hid2_mx = (hid2_codes, hid2_planes)
+
+        def hid2_sums(h, tag):
+            rows = sb("hid2_rows%d" % h, [P, PACK, HALF], BF16, tag=tag)
+            for t in range(PACK):
+                nc.vector.scalar_tensor_tensor(
+                    rows[:, t, :], ye[t][:, half_cols(h)], ye_gain[:, t : t + 1], wa[h][t][:], ALU.mult, ALU.add
+                )
+            woven = sb("hid2_%d" % h, [P, HALF, PACK], BF16)
+            nc.vector.tensor_copy(
+                woven[:].rearrange("p (c i) t -> p c t i", i=4), rows[:].rearrange("p t (c i) -> p c t i", i=4)
             )
-            if t < 2:
-                nc.vector.tensor_copy(x_codes[:, half_cols(t)], x_table[:].bitcast(U32).indirect(half_list(offs_t, t)))
+            return woven
+
+        def hid2_quantize(h, woven):
+            nc.vector.quantize_mx(
+                out=hid2_codes[:, half_cols(h)].bitcast(FP8X4),
+                scales=hid2_planes[:, half_cols(h)],
+                in_=woven[:].rearrange("p e t -> p (e t)"),
+            )
+
+        woven0 = hid2_sums(0, "w1_raw")
+        nc.vector.tensor_copy(x_codes[:, half_cols(0)], x_table[:].bitcast(U32).indirect(half_list(offs_t, 0)))
+        hid2_quantize(0, woven0)
+        nc.vector.tensor_copy(x_codes[:, half_cols(1)], x_table[:].bitcast(U32).indirect(half_list(offs_t, 1)))
+        woven1 = hid2_sums(1, "x_table")
 
         rect = []
         for h in range(2):
@@ -196,10 +229,6 @@ def tile_picked_ydrgtg_rel_p_kernel(
                     )
             rect.append(rows)
 
-        hid2 = sb("hid2", [P, Z, PACK], BF16)
-        nc.vector.tensor_copy(
-            hid2[:].rearrange("p (c i) t -> p c t i", i=4), hid2_rows[:].rearrange("p t (c i) -> p c t i", i=4)
-        )
         hid = []
         for h in range(2):
             both = sb("hid%d" % h, [P, P, PACK], BF16)
@@ -214,29 +243,48 @@ def tile_picked_ydrgtg_rel_p_kernel(
             )
 
         add_pair(0)
-        hid2_mx = quantize("hid2", hid2[:].rearrange("p e t -> p (e t)"), 1)
+        hid2_quantize(1, woven1)
         hid_mx = [quantize("hid0", hid[0][:].rearrange("p v t -> p (v t)"), 1)]
         add_pair(1)
         hid_mx.append(quantize("hid1", hid[1][:].rearrange("p v t -> p (v t)"), 1))
 
+        sc = [sb("sc%d" % h, [P, Z], F32) for h in range(2)]
+        for g in range(2):
+            acc = bank("b%d" % g, [P, HALF], "sc0_acc%d" % g)
+            product(acc[:], hid_mx[0], slice(0, P), hid2_mx, half_cols(g))
+            if g == 0:
+                nc.scalar.copy(sc[0][:, half_cols(g)], acc[:])
+            else:
+                nc.vector.tensor_copy(sc[0][:, half_cols(g)], acc[:])
+        acc = bank("b2", [P, Z], "sc1_acc")
+        product(acc[:], hid_mx[1], slice(0, P), hid2_mx, slice(0, Z))
+        nc.vector.tensor_copy(sc[1][:], acc[:])
+
+        allo, inv = [], []
         for h in range(2):
-            acc = bank("b%d" % h, [P, Z], "sc_acc%d" % h)
-            product(acc[:], hid_mx[h], slice(0, P), hid2_mx, slice(0, Z))
-            sc = sb("sc%d" % h, [P, Z], F32)
-            nc.scalar.copy(sc[:], acc[:])
             gate = sb("gate%d" % h, [P, Z], F32)
-            allo = sb("allo%d" % h, [P, Z], F32)
+            allo.append(sb("allo%d" % h, [P, Z], F32))
+            first = sb("first%d" % h, [P, 1], F32)
             for g in range(2):
-                nc.scalar.activation(gate[:, half_cols(g)], sc[:].indirect(half_list(alo_t, g)), ACT.Sigmoid)
-                nc.vector.tensor_tensor(allo[:, half_cols(g)], gate[:, half_cols(g)], sc[:, half_cols(g)], ALU.mult)
-            top = sb("top%d" % h, [P, 1], F32)
-            low = sb("low%d" % h, [P, 1], F32)
+                nc.scalar.activation(gate[:, half_cols(g)], sc[h][:].indirect(half_list(alo_t, g)), ACT.Sigmoid)
+                nc.vector.tensor_tensor(allo[h][:, half_cols(g)], gate[:, half_cols(g)], sc[h][:, half_cols(g)], ALU.mult)
+                if g == 0:
+                    nc.vector.tensor_reduce(first[:], allo[h][:, half_cols(0)], AXIS.X, ALU.max)
+            nc.vector.tensor_scalar(
+                gate[:, half_cols(1)], allo[h][:, half_cols(1)], first[:, 0:1], None, ALU.max, ALU.max,
+                accum_out=top_and_half[h][:, 0:1],
+            )
             den = sb("den%d" % h, [P, 1], F32)
-            inv = sb("inv%d" % h, [P, 1], F32)
-            nc.vector.tensor_reduce(top[:], allo[:], AXIS.X, ALU.max)
-            nc.vector.tensor_scalar(low[:], top[:], -1.0, 0.5, ALU.mult, ALU.add)
-            nc.vector.scalar_tensor_tensor(den[:], top[:], 0.5, low[:], ALU.add, ALU.max)
-            nc.vector.reciprocal(inv[:], den[:])
-            res = sb("res%d" % h, [P, Z], F32)
-            nc.vector.tensor_scalar(res[:], allo[:], inv[:, 0:1], None, ALU.mult)
-            nc.sync.dma_start(out[h * P : (h + 1) * P, :], res[:])
+            inv.append(sb("inv%d" % h, [P, 1], F32))
+            nc.vector.tensor_reduce(den[:], top_and_half[h][:], AXIS.X, ALU.add, apply_absolute_value=True)
+            nc.vector.reciprocal(inv[h][:], den[:])
+
+        res0 = sb("res0", [P, Z], F32)
+        nc.scalar.activation(res0[:], allo[0][:], ACT.Copy, scale=inv[0][:, 0:1])
+        nc.sync.dma_start(out[0:P, :], res0[:])
+        res1a = sb("res1a", [P, HALF], F32)
+        res1b = sb("res1b", [P, HALF], F32)
+        nc.vector.tensor_scalar(res1a[:], allo[1][:, half_cols(0)], inv[1][:, 0:1], None, ALU.mult)
+        nc.sync.dma_start(out[P : 2 * P, half_cols(0)], res1a[:])
+        nc.scalar.activation(res1b[:], allo[1][:, half_cols(1)], ACT.Copy, scale=inv[1][:, 0:1])
+        nc.scalar.dma_start(out[P : 2 * P, half_cols(1)], res1b[:])

@@ -20,6 +20,7 @@ P = 128
 PACK = 4
 HALF = 256
 LIST_COLS = HALF // 16
+X_ROW = 4
 
 FLOPS = 2 * K * H * (S + 2 * Z) + 2 * H * V * Z
 
@@ -48,11 +49,11 @@ def tile_picked_ydrgtg_rel_p_kernel(
             nc.sync.dma_start(tile[:], src[0].rearrange("p n t -> p (n t)").bitcast(I32))
             return tile
 
-        def load_scales(name, src, width, queue):
+        def load_scales(name, src, width, row0):
             tile = sb(name, [P, width], U8)
             nc.gpsimd.memset(tile[:].bitcast(I32), 0)
-            for q in range(4):
-                queue.dma_start(tile[32 * q : 32 * q + 4, :].bitcast(I32), src[0, 4 * q : 4 * q + 4, :].bitcast(I32))
+            for r in range(4):
+                nc.sync.dma_start(tile[row0 + r : P : 32, :].bitcast(I32), src[0, r:16:4, :].bitcast(I32))
             return tile
 
         def load_weight(name, src):
@@ -88,13 +89,13 @@ def tile_picked_ydrgtg_rel_p_kernel(
                 )
             return codes, scales
 
-        def product(dst, stat, stat_cols, mov, mov_cols):
+        def product(dst, stat, stat_cols, mov, mov_cols, row0=0):
             nc.tensor.matmul_mx(
                 out=dst,
                 lhsT=stat[0][:, stat_cols].bitcast(FP8X4),
                 lhsT_scale=stat[1][:, stat_cols],
                 rhs=mov[0][:, mov_cols].bitcast(FP8X4),
-                rhs_scale=mov[1][:, mov_cols],
+                rhs_scale=mov[1][row0:P, mov_cols],
                 start=True,
                 stop=True,
             )
@@ -108,14 +109,14 @@ def tile_picked_ydrgtg_rel_p_kernel(
         def half_list(tile, h):
             return tile[:, h * LIST_COLS : (h + 1) * LIST_COLS]
 
+        e_table = load_words("e_table", e_words, W)
         pok_t = load_list("pok_t", pok)
         offs_t = load_list("offs_t", offs)
-        e_table = load_words("e_table", e_words, W)
-        e_bytes = load_scales("e_bytes", e_scales, W, nc.sync)
+        e_bytes = load_scales("e_bytes", e_scales, W, 0)
         w3_raw = load_weight("w3_raw", w3)
         unit_t = load_unit("unit_t", unit)
         unit2_t = load_unit("unit2_t", unit2)
-        x_bytes = load_scales("x_bytes", x_scales, T, nc.sync)
+        x_bytes = load_scales("x_bytes", x_scales, T, X_ROW)
         w2_raw = load_weight("w2_raw", w2)
         adj_t = load_list("adj_t", adj)
         w1_raw = load_weight("w1_raw", w1)
@@ -181,21 +182,21 @@ def tile_picked_ydrgtg_rel_p_kernel(
                 wa[h].append(rows)
 
         w1_dealt = deal_weight("w1_dealt", w1_raw, 0)
-        w1_mx = quantize("w1", w1_dealt[:].rearrange("p t m j -> p (t m j)"), 1)
-
         hid2_codes = sb("hid2_codes", [P, Z], U32)
         hid2_planes = sb("hid2_planes", [P, Z], U8)
         hid2_mx = (hid2_codes, hid2_planes)
+        hid2_rows = [sb("hid2_rows0", [P, PACK, HALF], BF16, tag="w1_raw"), None]
 
-        def hid2_sums(h, tag):
-            rows = sb("hid2_rows%d" % h, [P, PACK, HALF], BF16, tag=tag)
-            for t in range(PACK):
-                nc.vector.scalar_tensor_tensor(
-                    rows[:, t, :], ye[t][:, half_cols(h)], ye_gain[:, t : t + 1], wa[h][t][:], ALU.mult, ALU.add
-                )
+        def hid2_sum(h, t):
+            nc.vector.scalar_tensor_tensor(
+                hid2_rows[h][:, t, :], ye[t][:, half_cols(h)], ye_gain[:, t : t + 1], wa[h][t][:], ALU.mult, ALU.add
+            )
+
+        def hid2_weave(h):
             woven = sb("hid2_%d" % h, [P, HALF, PACK], BF16)
             nc.vector.tensor_copy(
-                woven[:].rearrange("p (c i) t -> p c t i", i=4), rows[:].rearrange("p t (c i) -> p c t i", i=4)
+                woven[:].rearrange("p (c i) t -> p c t i", i=4),
+                hid2_rows[h][:].rearrange("p t (c i) -> p c t i", i=4),
             )
             return woven
 
@@ -206,11 +207,18 @@ def tile_picked_ydrgtg_rel_p_kernel(
                 in_=woven[:].rearrange("p e t -> p (e t)"),
             )
 
-        woven0 = hid2_sums(0, "w1_raw")
-        nc.vector.tensor_copy(x_codes[:, half_cols(0)], x_table[:].bitcast(U32).indirect(half_list(offs_t, 0)))
+        hid2_sum(0, 0)
+        w1_mx = quantize("w1", w1_dealt[:].rearrange("p t m j -> p (t m j)"), 1)
+        for h in range(2):
+            nc.vector.tensor_copy(x_codes[:, half_cols(h)], x_table[:].bitcast(U32).indirect(half_list(offs_t, h)))
+        for t in range(1, PACK):
+            hid2_sum(0, t)
+        hid2_rows[1] = sb("hid2_rows1", [P, PACK, HALF], BF16, tag="x_table")
+        for t in range(PACK):
+            hid2_sum(1, t)
+        woven0 = hid2_weave(0)
+        woven1 = hid2_weave(1)
         hid2_quantize(0, woven0)
-        nc.vector.tensor_copy(x_codes[:, half_cols(1)], x_table[:].bitcast(U32).indirect(half_list(offs_t, 1)))
-        woven1 = hid2_sums(1, "x_table")
 
         rect = []
         for h in range(2):
@@ -218,7 +226,7 @@ def tile_picked_ydrgtg_rel_p_kernel(
             for pair in range(2):
                 acc = bank("a%d" % (2 * h + pair), [P, 2, HALF], "y_acc%d" % (2 * h + pair))
                 for u in range(2):
-                    product(acc[:, u, :], w1_mx, tile_cols(2 * pair + u), x_mx, half_cols(h))
+                    product(acc[:, u, :], w1_mx, tile_cols(2 * pair + u), x_mx, half_cols(h), X_ROW)
                 for u in range(2):
                     t = 2 * pair + u
                     nc.scalar.activation(
@@ -252,32 +260,44 @@ def tile_picked_ydrgtg_rel_p_kernel(
         for g in range(2):
             acc = bank("b%d" % g, [P, HALF], "sc0_acc%d" % g)
             product(acc[:], hid_mx[0], slice(0, P), hid2_mx, half_cols(g))
-            if g == 0:
-                nc.scalar.copy(sc[0][:, half_cols(g)], acc[:])
-            else:
-                nc.vector.tensor_copy(sc[0][:, half_cols(g)], acc[:])
+            nc.scalar.copy(sc[0][:, half_cols(g)], acc[:])
         acc = bank("b2", [P, Z], "sc1_acc")
         product(acc[:], hid_mx[1], slice(0, P), hid2_mx, slice(0, Z))
         nc.vector.tensor_copy(sc[1][:], acc[:])
 
-        allo, inv = [], []
-        for h in range(2):
-            gate = sb("gate%d" % h, [P, Z], F32)
-            allo.append(sb("allo%d" % h, [P, Z], F32))
-            first = sb("first%d" % h, [P, 1], F32)
-            for g in range(2):
-                nc.scalar.activation(gate[:, half_cols(g)], sc[h][:].indirect(half_list(alo_t, g)), ACT.Sigmoid)
-                nc.vector.tensor_tensor(allo[h][:, half_cols(g)], gate[:, half_cols(g)], sc[h][:, half_cols(g)], ALU.mult)
-                if g == 0:
-                    nc.vector.tensor_reduce(first[:], allo[h][:, half_cols(0)], AXIS.X, ALU.max)
+        gate = [sb("gate%d" % h, [P, Z], F32) for h in range(2)]
+        allo = [sb("allo%d" % h, [P, Z], F32) for h in range(2)]
+        den = [sb("den%d" % h, [P, 1], F32) for h in range(2)]
+        inv = [sb("inv%d" % h, [P, 1], F32) for h in range(2)]
+        first = [sb("first%d" % h, [P, 1], F32) for h in range(2)]
+
+        def gated(h, a, b):
+            nc.scalar.activation(gate[h][:, a:b], sc[h][:].indirect(alo_t[:, a // 16 : b // 16]), ACT.Sigmoid)
+            nc.vector.tensor_tensor(allo[h][:, a:b], gate[h][:, a:b], sc[h][:, a:b], ALU.mult)
+
+        def largest(dst, h, a, b):
+            nc.vector.tensor_reduce(dst, allo[h][:, a:b], AXIS.X, ALU.max)
+
+        def inverse(h):
+            nc.vector.tensor_reduce(den[h][:], top_and_half[h][:], AXIS.X, ALU.add, apply_absolute_value=True)
+            nc.vector.reciprocal(inv[h][:], den[h][:])
+
+        def last(h, a):
             nc.vector.tensor_scalar(
-                gate[:, half_cols(1)], allo[h][:, half_cols(1)], first[:, 0:1], None, ALU.max, ALU.max,
+                gate[h][:, a:Z], allo[h][:, a:Z], first[h][:, 0:1], None, ALU.max, ALU.max,
                 accum_out=top_and_half[h][:, 0:1],
             )
-            den = sb("den%d" % h, [P, 1], F32)
-            inv.append(sb("inv%d" % h, [P, 1], F32))
-            nc.vector.tensor_reduce(den[:], top_and_half[h][:], AXIS.X, ALU.add, apply_absolute_value=True)
-            nc.vector.reciprocal(inv[h][:], den[:])
+
+        gated(0,0,256)
+        largest(first[0][:],0,0,256)
+        gated(0,256,512)
+        last(0,256)
+        inverse(0)
+        gated(1,0,256)
+        largest(first[1][:],1,0,256)
+        gated(1,256,512)
+        last(1,256)
+        inverse(1)
 
         res0 = sb("res0", [P, Z], F32)
         nc.scalar.activation(res0[:], allo[0][:], ACT.Copy, scale=inv[0][:, 0:1])
@@ -286,5 +306,5 @@ def tile_picked_ydrgtg_rel_p_kernel(
         res1b = sb("res1b", [P, HALF], F32)
         nc.vector.tensor_scalar(res1a[:], allo[1][:, half_cols(0)], inv[1][:, 0:1], None, ALU.mult)
         nc.sync.dma_start(out[P : 2 * P, half_cols(0)], res1a[:])
-        nc.scalar.activation(res1b[:], allo[1][:, half_cols(1)], ACT.Copy, scale=inv[1][:, 0:1])
+        nc.vector.tensor_scalar(res1b[:], allo[1][:, half_cols(1)], inv[1][:, 0:1], None, ALU.mult)
         nc.scalar.dma_start(out[P : 2 * P, half_cols(1)], res1b[:])

from contextlib import ExitStack

import concourse.mybir as mybir

K, T, S, H, Z, W = 512, 2048, 512, 512, 512, 1024
V = S // 2

F32 = mybir.dt.float32
BF16 = mybir.dt.bfloat16
I32 = mybir.dt.int32
U32 = mybir.dt.uint32
U16 = mybir.dt.uint16
U8 = mybir.dt.uint8
FP8X4 = mybir.dt.float8_e4m3fn_x4
ALU = mybir.AluOpType
ACT = mybir.ActivationFunctionType
AXIS = mybir.AxisListType

P = 128
PACK = 4
HALF = 256
LIST_COLS = HALF // 16
X_ROW = 4

FLOPS = 2 * K * H * (S + 2 * Z) + 2 * H * V * Z


def tile_picked_ydrgtg_rel_p_kernel(
    tc, x_words, x_scales, w1, e_words, e_scales, w2, w3, unit, unit2, offs, pok, adj, alo, out
):
    nc = tc.nc
    with ExitStack() as ctx:
        keep = ctx.enter_context(tc.tile_pool(name="keep", bufs=1))
        psum = ctx.enter_context(tc.psum_pool(name="psum", bufs=1))

        def sb(name, shape, dtype, tag=""):
            return keep.tile(shape, dtype, name=name, tag=tag or name, align_bytes=64)

        def bank(tag, shape, name):
            return psum.tile(shape, F32, name=name, tag=tag)

        def load_list(name, src):
            tile = keep.tile([P, 32], U16, name=name)
            nc.sync.dma_start(tile[:], src)
            return tile

        def load_words(name, src, width):
            tile = sb(name, [P, width], I32)
            nc.sync.dma_start(tile[:], src[0].rearrange("p n t -> p (n t)").bitcast(I32))
            return tile

        def load_scales(name, src, width, row0):
            tile = sb(name, [P, width], U8)
            nc.gpsimd.memset(tile[:].bitcast(I32), 0)
            for r in range(4):
                nc.sync.dma_start(tile[row0 + r : P : 32, :].bitcast(I32), src[0, r:16:4, :].bitcast(I32))
            return tile

        def load_weight(name, src):
            tile = sb(name, [P, PACK, H], F32)
            nc.sync.dma_start(tile[:], src.rearrange("(p j) c -> p j c", j=PACK))
            return tile

        def load_unit(name, src):
            tile = sb(name, [P, PACK], F32)
            nc.sync.dma_start(tile[:], src.rearrange("(p t) o -> p (t o)", t=PACK))
            return tile

        def deal_weight(name, raw, scalar_cols):
            dealt = sb(name, [P, PACK, P, PACK], BF16)
            dst = dealt[:].rearrange("p t m j -> p m j t")
            src = raw[:].rearrange("p j (m t) -> p m j t", t=PACK)
            if scalar_cols > 0:
                nc.scalar.copy(dst[:, :scalar_cols], src[:, :scalar_cols])
            if scalar_cols < P:
                nc.vector.tensor_copy(dst[:, scalar_cols:], src[:, scalar_cols:])
            return dealt

        def quantize(name, flat, pieces):
            width = flat.shape[1] // PACK
            codes = sb(name + "_codes", [P, width], U32)
            scales = sb(name + "_scales", [P, width], U8)
            step = width // pieces
            for c in range(0, width, step):
                nc.vector.quantize_mx(
                    out=codes[:, c : c + step].bitcast(FP8X4),
                    scales=scales[:, c : c + step],
                    in_=flat[:, PACK * c : PACK * (c + step)],
                )
            return codes, scales

        def product(dst, stat, stat_cols, mov, mov_cols, row0=0):
            nc.tensor.matmul_mx(
                out=dst,
                lhsT=stat[0][:, stat_cols].bitcast(FP8X4),
                lhsT_scale=stat[1][:, stat_cols],
                rhs=mov[0][:, mov_cols].bitcast(FP8X4),
                rhs_scale=mov[1][row0:P, mov_cols],
                start=True,
                stop=True,
            )

        def tile_cols(t):
            return slice(t * P, (t + 1) * P)

        def half_cols(h):
            return slice(h * HALF, (h + 1) * HALF)

        def half_list(tile, h):
            return tile[:, h * LIST_COLS : (h + 1) * LIST_COLS]

        e_table = load_words("e_table", e_words, W)
        pok_t = load_list("pok_t", pok)
        offs_t = load_list("offs_t", offs)
        e_bytes = load_scales("e_bytes", e_scales, W, 0)
        w3_raw = load_weight("w3_raw", w3)
        unit_t = load_unit("unit_t", unit)
        unit2_t = load_unit("unit2_t", unit2)
        x_bytes = load_scales("x_bytes", x_scales, T, X_ROW)
        w2_raw = load_weight("w2_raw", w2)
        adj_t = load_list("adj_t", adj)
        w1_raw = load_weight("w1_raw", w1)
        x_table = load_words("x_table", x_words, T)
        alo_t = load_list("alo_t", alo)

        warm_in = sb("warm_in", [P, 1], F32)
        warm_out = sb("warm_out", [P, 1], F32)
        nc.gpsimd.memset(warm_in[:], 0.0)
        nc.scalar.activation(warm_out[:], warm_in[:], ACT.Sigmoid)

        step01 = sb("step01", [P, PACK], F32)
        sign = sb("sign", [P, PACK], F32)
        unit_abs = sb("unit_abs", [P, PACK], F32)
        ye_gain = sb("ye_gain", [P, PACK], F32)
        yw_gain = sb("yw_gain", [P, PACK], F32)
        sign07 = sb("sign07", [P, PACK], F32)
        nc.gpsimd.tensor_scalar(step01[:], unit_t[:], 0.0, None, ALU.is_ge)
        nc.gpsimd.tensor_scalar(sign07[:], step01[:], -1.4, 0.7, ALU.mult, ALU.add)
        nc.gpsimd.tensor_tensor(yw_gain[:], unit2_t[:], sign07[:], ALU.mult)
        nc.gpsimd.tensor_scalar(sign[:], step01[:], 2.0, -1.0, ALU.mult, ALU.add)
        nc.gpsimd.tensor_tensor(ye_gain[:], unit2_t[:], sign[:], ALU.mult)
        nc.scalar.activation(unit_abs[:], unit_t[:], ACT.Abs)
        top_and_half = []
        for h in range(2):
            pair = sb("top_and_half%d" % h, [P, 2], F32)
            nc.vector.memset(pair[:], 0.5)
            top_and_half.append(pair)

        e_codes = sb("e_codes", [P, Z], U32)
        e_planes = sb("e_planes", [P, Z], U8)
        nc.vector.tensor_copy(e_codes[:], e_table[:].bitcast(U32).indirect(pok_t[:]))
        nc.vector.tensor_copy(e_planes[:], e_bytes[:].indirect(pok_t[:]))
        e_mx = (e_codes, e_planes)
        x_codes = sb("x_codes", [P, S], U32)
        x_planes = sb("x_planes", [P, S], U8)
        x_mx = (x_codes, x_planes)

        w3_dealt = deal_weight("w3_dealt", w3_raw, 44)
        w3_mx = quantize("w3", w3_dealt[:].rearrange("p t m j -> p (t m j)"), 2)
        yw = []
        for t in range(PACK):
            acc = bank("a%d" % t, [P, Z], "yw_acc%d" % t)
            product(acc[:], w3_mx, tile_cols(t), e_mx, slice(0, Z))
            rows = sb("yw%d" % t, [P, Z], F32)
            nc.scalar.activation(rows[:], acc[:], ACT.Copy, scale=yw_gain[:, t : t + 1])
            yw.append(rows)

        nc.vector.tensor_copy(x_planes[:], x_bytes[:].indirect(offs_t[:]))
        w2_dealt = deal_weight("w2_dealt", w2_raw, 0)
        w2_mx = quantize("w2", w2_dealt[:].rearrange("p t m j -> p (t m j)"), 1)
        ye = []
        for t in range(PACK):
            acc = bank("b%d" % t, [P, Z], "ye_acc%d" % t)
            product(acc[:], w2_mx, tile_cols(t), e_mx, slice(0, Z))
            ye.append(acc)

        wa = [[], []]
        for h in range(2):
            for t in range(PACK):
                rows = sb("wa%d_%d" % (h, t), [P, HALF], F32)
                nc.scalar.activation(rows[:], yw[t][:].indirect(half_list(adj_t, h)), ACT.Copy)
                wa[h].append(rows)

        w1_dealt = deal_weight("w1_dealt", w1_raw, 0)
        hid2_codes = sb("hid2_codes", [P, Z], U32)
        hid2_planes = sb("hid2_planes", [P, Z], U8)
        hid2_mx = (hid2_codes, hid2_planes)
        hid2_rows = [sb("hid2_rows0", [P, PACK, HALF], BF16, tag="w1_raw"), None]

        def hid2_sum(h, t):
            nc.vector.scalar_tensor_tensor(
                hid2_rows[h][:, t, :], ye[t][:, half_cols(h)], ye_gain[:, t : t + 1], wa[h][t][:], ALU.mult, ALU.add
            )

        def hid2_weave(h):
            woven = sb("hid2_%d" % h, [P, HALF, PACK], BF16)
            nc.vector.tensor_copy(
                woven[:].rearrange("p (c i) t -> p c t i", i=4),
                hid2_rows[h][:].rearrange("p t (c i) -> p c t i", i=4),
            )
            return woven

        def hid2_quantize(h, woven):
            nc.vector.quantize_mx(
                out=hid2_codes[:, half_cols(h)].bitcast(FP8X4),
                scales=hid2_planes[:, half_cols(h)],
                in_=woven[:].rearrange("p e t -> p (e t)"),
            )

        hid2_sum(0, 0)
        w1_mx = quantize("w1", w1_dealt[:].rearrange("p t m j -> p (t m j)"), 1)
        for h in range(2):
            nc.vector.tensor_copy(x_codes[:, half_cols(h)], x_table[:].bitcast(U32).indirect(half_list(offs_t, h)))
        for t in range(1, PACK):
            hid2_sum(0, t)
        hid2_rows[1] = sb("hid2_rows1", [P, PACK, HALF], BF16, tag="x_table")
        for t in range(PACK):
            hid2_sum(1, t)
        woven0 = hid2_weave(0)
        woven1 = hid2_weave(1)
        hid2_quantize(0, woven0)

        rect = []
        for h in range(2):
            rows = sb("rect%d" % h, [P, 2, PACK, P], F32)
            for pair in range(2):
                acc = bank("a%d" % (2 * h + pair), [P, 2, HALF], "y_acc%d" % (2 * h + pair))
                for u in range(2):
                    product(acc[:, u, :], w1_mx, tile_cols(2 * pair + u), x_mx, half_cols(h), X_ROW)
                for u in range(2):
                    t = 2 * pair + u
                    nc.scalar.activation(
                        rows[:, :, t, :],
                        acc[:, u, :].rearrange("p (v d) -> p d v", d=2),
                        ACT.Relu,
                        scale=unit_abs[:, t : t + 1],
                    )
            rect.append(rows)

        hid = []
        for h in range(2):
            both = sb("hid%d" % h, [P, P, PACK], BF16)
            hid.append(both)

        def add_pair(h):
            nc.vector.tensor_tensor(
                hid[h][:].rearrange("p (c i) t -> p c t i", i=4),
                rect[h][:, 0].rearrange("p t (c i) -> p c t i", i=4),
                rect[h][:, 1].rearrange("p t (c i) -> p c t i", i=4),
                ALU.add,
            )

        add_pair(0)
        hid2_quantize(1, woven1)
        hid_mx = [quantize("hid0", hid[0][:].rearrange("p v t -> p (v t)"), 1)]
        add_pair(1)
        hid_mx.append(quantize("hid1", hid[1][:].rearrange("p v t -> p (v t)"), 1))

        sc = [sb("sc%d" % h, [P, Z], F32) for h in range(2)]
        for g in range(2):
            acc = bank("b%d" % g, [P, HALF], "sc0_acc%d" % g)
            product(acc[:], hid_mx[0], slice(0, P), hid2_mx, half_cols(g))
            nc.scalar.copy(sc[0][:, half_cols(g)], acc[:])
        acc = bank("b2", [P, Z], "sc1_acc")
        product(acc[:], hid_mx[1], slice(0, P), hid2_mx, slice(0, Z))
        nc.vector.tensor_copy(sc[1][:], acc[:])

        gate = [sb("gate%d" % h, [P, Z], F32) for h in range(2)]
        allo = [sb("allo%d" % h, [P, Z], F32) for h in range(2)]
        den = [sb("den%d" % h, [P, 1], F32) for h in range(2)]
        inv = [sb("inv%d" % h, [P, 1], F32) for h in range(2)]
        first = [sb("first%d" % h, [P, 1], F32) for h in range(2)]

        def gated(h, a, b):
            nc.scalar.activation(gate[h][:, a:b], sc[h][:].indirect(alo_t[:, a // 16 : b // 16]), ACT.Sigmoid)
            nc.vector.tensor_tensor(allo[h][:, a:b], gate[h][:, a:b], sc[h][:, a:b], ALU.mult)

        def largest(dst, h, a, b):
            nc.vector.tensor_reduce(dst, allo[h][:, a:b], AXIS.X, ALU.max)

        def inverse(h):
            nc.vector.tensor_reduce(den[h][:], top_and_half[h][:], AXIS.X, ALU.add, apply_absolute_value=True)
            nc.vector.reciprocal(inv[h][:], den[h][:])

        def last(h, a):
            nc.vector.tensor_scalar(
                gate[h][:, a:Z], allo[h][:, a:Z], first[h][:, 0:1], None, ALU.max, ALU.max,
                accum_out=top_and_half[h][:, 0:1],
            )

        gated(0,0,256)
        largest(first[0][:],0,0,256)
        gated(0,256,512)
        last(0,256)
        inverse(0)
        gated(1,0,256)
        largest(first[1][:],1,0,256)
        gated(1,256,512)
        last(1,256)
        inverse(1)

        res0 = sb("res0", [P, Z], F32)
        nc.scalar.activation(res0[:], allo[0][:], ACT.Copy, scale=inv[0][:, 0:1])
        nc.sync.dma_start(out[0:P, :], res0[:])
        res1a = sb("res1a", [P, HALF], F32)
        res1b = sb("res1b", [P, HALF], F32)
        nc.vector.tensor_scalar(res1a[:], allo[1][:, half_cols(0)], inv[1][:, 0:1], None, ALU.mult)
        nc.sync.dma_start(out[P : 2 * P, half_cols(0)], res1a[:])
        nc.vector.tensor_scalar(res1b[:], allo[1][:, half_cols(1)], inv[1][:, 0:1], None, ALU.mult)
        nc.scalar.dma_start(out[P : 2 * P, half_cols(1)], res1b[:])
